import numpy as np
import ml_dtypes


def mxq(x, axis, fmt="e4m3"):
    dtype, down = {"e4m3": (ml_dtypes.float8_e4m3fn, 7), "e5m2": (ml_dtypes.float8_e5m2, 14)}[fmt]
    v = np.moveaxis(np.asarray(x, np.float32).astype(ml_dtypes.bfloat16).astype(np.float64), axis, -1)
    blocks = v.reshape(v.shape[:-1] + (-1, 32))
    amax = np.abs(blocks).max(-1, keepdims=True)
    byte = np.maximum(np.where(amax > 0, np.frexp(amax)[1] - 1 + 127, 0) - down, 1)
    scale = np.exp2(byte - 127.0)
    codes = (blocks / scale).astype(np.float32).astype(dtype).astype(np.float64)
    return np.moveaxis((codes * scale).reshape(v.shape), -1, axis)


WIDE = False


def mx_kscale(k):
    if not WIDE:
        return np.ones(k)
    levels = np.array([10, -10, 5, -5, 0])
    if k % 512:
        return np.exp2(np.random.permutation(np.resize(levels, k // 32))).repeat(32)
    a = np.empty((k // 512, 16))
    for p in range(k // 512):
        a[p, :8] = np.random.permutation(np.resize(levels, 8))
        for g in range(8):
            far = levels[np.abs(levels - a[p, g]) >= 10]
            a[p, g + 8] = far[np.random.randint(len(far))]
    return np.exp2(a.ravel()).repeat(32)


def f64(x):
    return np.asarray(x).astype(np.float64)


def striped(idx):
    return np.tile(idx.reshape(-1, 16).T, (8, 1)).astype(np.uint16)


def unstriped(offs):
    return offs[:16].T.reshape(-1).astype(np.int64)


def striped8(idx):
    return np.concatenate([x.reshape(-1, 16).T for x in idx]).astype(np.uint16)


def runs(offs, k):
    lists = np.stack([offs[16 * r : 16 * r + 16].T.reshape(-1) for r in range(8)]).astype(np.int64)
    return lists[np.arange(k) % 512 // 64]


def pack_weight(w):
    k, n = w.shape
    w = f64(np.asarray(w, np.float32).astype(ml_dtypes.bfloat16)).reshape(k // 32, 32, n)
    amax = np.abs(w).max(1)
    byte = np.clip(np.where(amax > 0, np.frexp(amax)[1] - 1 + 127 - 7, 1), 1, 254)
    scaled = (w * np.exp2(127.0 - byte)[:, None, :]).reshape(k, n).astype(np.float32)
    words = np.ascontiguousarray(scaled.reshape(k // 512, 128, 4, n).transpose(0, 1, 3, 2)).astype(ml_dtypes.float8_e4m3fn).view(np.uint8)
    return words, np.ascontiguousarray(byte.astype(np.uint8).reshape(k // 512, 16, n))


def unpack_weight(words, scales):
    g, p, n, _ = words.shape
    vals = np.ascontiguousarray(words).view(ml_dtypes.float8_e4m3fn).astype(np.float64) * np.repeat(np.exp2(scales.astype(np.float64) - 127.0), 8, axis=1)[..., None]
    return vals.transpose(0, 1, 3, 2).reshape(g * 512, n)


def sigmoid(v):
    return 1.0 / (1.0 + np.exp(-np.maximum(v, -700.0)))

def planes(y):
    n, m = y.shape
    v = y.astype(np.float32).astype(ml_dtypes.bfloat16).astype(np.float64).reshape(n // 32, 32, m)
    top = np.abs(v).max(1)
    byte = np.clip(np.where(top > 0, np.frexp(top)[1] - 1 + 127 - 7, 1), 1, 254)
    codes = (v * np.exp2(127.0 - byte)[:, None, :]).reshape(n, m).astype(np.float32).astype(ml_dtypes.float8_e4m3fn).view(np.uint8)
    words = codes.reshape(n // 512, 128, 4, m).transpose(0, 1, 3, 2)
    return np.ascontiguousarray(words), np.ascontiguousarray(byte.astype(np.uint8).reshape(n // 512, 16, m))


K, T, S, N, H, G = 512, 2048, 512, 512, 512, 2048


def setup_inputs():
    n = np.random.standard_normal
    s = mx_kscale(K)[:, None]
    u = mx_kscale(H)
    packed_xT = pack_weight(n((K, T)) * s)
    packed_w1 = pack_weight(n((K, H)) / np.sqrt(K) / s)
    packed_dT = pack_weight(n((K, G)) / s)
    packed_w2 = pack_weight(n((H, N)) / np.sqrt(H) / u[:, None])
    return {
        "x_words": packed_xT[0],
        "x_scales": packed_xT[1],
        "w1_words": packed_w1[0],
        "w1_scales": packed_w1[1],
        "gs": (np.random.uniform(0.5, 1.5, (K, 1)) * s).astype(np.float32),
        "d_words": packed_dT[0],
        "d_scales": packed_dT[1],
        "gn": (np.random.uniform(0.5, 1.5, (H, 1)) * u[:, None]).astype(np.float32),
        "res": n((N, S)).astype(np.float32),
        "w2_words": packed_w2[0],
        "w2_scales": packed_w2[1],
        "offs": striped(np.random.permutation(T)[:S]),
        "nb": striped8(np.stack([np.random.permutation(S) for _ in range(8)])),
        "kidx": striped8(np.random.randint(0, G, (8, H))),
    }


def reference(x_words, x_scales, w1_words, w1_scales, gs, d_words, d_scales, gn, res, w2_words, w2_scales, offs, nb, kidx):
    d_kidx = unpack_weight(d_words, d_scales)[np.arange(K)[:, None], runs(kidx, K)]
    xq = unpack_weight(x_words, x_scales)[:, unstriped(offs)]
    y = unpack_weight(w1_words, w1_scales).T @ xq
    zq = f64(gs) * (y - (y[np.arange(H)[:, None], runs(nb, H)]))
    s = 0.0625 * ((d_kidx.T @ mxq(zq, 0, "e4m3")))
    z2 = f64(gn) * sigmoid(s)
    out_0 = f64(res) + (unpack_weight(w2_words, w2_scales).T @ mxq(z2, 0, "e4m3"))
    return (out_0,) + planes(out_0)

@@ -1,0 +1,230 @@
+from contextlib import ExitStack
+
+import concourse.mybir as mybir
+
+K, T, S, N, H, G = 512, 2048, 512, 512, 512, 2048
+FLOPS = 3 * 2 * 512 * 512 * 512
+
+F32 = mybir.dt.float32
+BF16 = mybir.dt.bfloat16
+I32 = mybir.dt.int32
+U32 = mybir.dt.uint32
+U16 = mybir.dt.uint16
+U8 = mybir.dt.uint8
+FP8X4 = mybir.dt.float8_e4m3fn_x4
+ACT = mybir.ActivationFunctionType
+ALU = mybir.AluOpType
+
+P = 128
+PACK = 4
+CH = 128
+CHUNKS = S // CH
+LIST_COLS = CH // 16
+
+
+def words_of(dram):
+    return dram[0].rearrange("p n t -> p (n t)").bitcast(I32)
+
+
+def scale_rows(dram, r):
+    return dram[0].rearrange("(q r) c -> r q c", r=PACK)[r].bitcast(I32)
+
+
+def deal(nc, dealt, plain, run):
+    nc.vector.tensor_copy(
+        out=dealt.rearrange("p (t c i) -> p c t i", t=PACK, i=run),
+        in_=plain.rearrange("p (c i t) -> p c t i", t=PACK, i=run),
+    )
+
+
+def weave(nc, woven, planes, scale):
+    nc.scalar.activation(
+        out=woven[:].rearrange("p (c i) t -> p c t i", i=4),
+        in_=planes.rearrange("p t (c i) -> p c t i", i=4),
+        func=ACT.Copy,
+        scale=scale,
+    )
+
+
+def tile_picked_pqhop_sigmoid_po_kernel(
+    tc, x_words, x_scales, w1_words, w1_scales, gs, d_words, d_scales, gn, res, w2_words, w2_scales, offs, nb, kidx,
+    out_0, out_1, out_2,
+):
+    nc = tc.nc
+    with ExitStack() as ctx:
+        lists = ctx.enter_context(tc.tile_pool(name="lists", bufs=1))
+        keep = ctx.enter_context(tc.tile_pool(name="keep", bufs=1))
+        ring = ctx.enter_context(tc.tile_pool(name="ring", bufs=CHUNKS))
+        ybank = ctx.enter_context(tc.psum_pool(name="ybank", bufs=PACK))
+        sbank = ctx.enter_context(tc.psum_pool(name="sbank", bufs=2))
+        obank = ctx.enter_context(tc.psum_pool(name="obank", bufs=2))
+
+        offs_t = lists.tile([P, S // 16], U16, name="offs_t")
+        kidx_t = lists.tile([P, H // 16], U16, name="kidx_t")
+        nb_t = lists.tile([P, S // 16], U16, name="nb_t")
+
+        xs_tab = keep.tile([P, T], U8, align_bytes=64, name="xs_tab")
+        ds_tab = keep.tile([P, G], U8, align_bytes=64, name="ds_tab")
+        xw_tab = keep.tile([P, T], U32, align_bytes=64, name="xw_tab")
+        dw_tab = keep.tile([P, G], U32, align_bytes=64, name="dw_tab")
+        w1w_raw = keep.tile([P, H], I32, align_bytes=64, name="w1w_raw")
+        w1s_raw = keep.tile([P, H], U8, align_bytes=64, name="w1s_raw")
+        w2w_raw = keep.tile([P, N], I32, align_bytes=64, name="w2w_raw")
+        w2s_raw = keep.tile([P, N], U8, align_bytes=64, name="w2s_raw")
+        ds_fin = keep.tile([P, H], U8, align_bytes=64, name="ds_fin")
+        gs_t = keep.tile([P, PACK], F32, name="gs_t")
+        gn_t = keep.tile([P, PACK], F32, name="gn_t")
+        res_t = keep.tile([P, PACK, S], F32, name="res_t")
+        warm_in = keep.tile([P, 1], F32, name="warm_in")
+        warm_out = keep.tile([P, 1], F32, name="warm_out")
+
+        nc.gpsimd.memset(xs_tab[:].bitcast(I32), 0)
+        nc.vector.memset(ds_tab[:].bitcast(I32), 0)
+        nc.vector.memset(warm_in[:], 0.0)
+        nc.vector.memset(w1s_raw[:].bitcast(I32), 0)
+        nc.vector.memset(w2s_raw[:].bitcast(I32), 0)
+        nc.vector.memset(ds_fin[:].bitcast(I32), 0)
+        nc.scalar.activation(out=warm_out[:], in_=warm_in[:], func=ACT.Sigmoid)
+
+        nc.sync.dma_start(offs_t[:], offs)
+        for r in range(PACK):
+            nc.sync.dma_start(xs_tab[r:P:32, :].bitcast(I32), scale_rows(x_scales, r))
+        nc.sync.dma_start(kidx_t[:], kidx)
+        nc.sync.dma_start(ds_tab[0:P:8, :].bitcast(I32), d_scales[0].bitcast(I32))
+        nc.sync.dma_start(xw_tab[:].bitcast(I32), words_of(x_words))
+        nc.sync.dma_start(w1w_raw[:], words_of(w1_words))
+        for r in range(PACK):
+            nc.sync.dma_start(w1s_raw[r:P:32, :].bitcast(I32), scale_rows(w1_scales, r))
+        nc.sync.dma_start(dw_tab[:].bitcast(I32), words_of(d_words))
+        nc.sync.dma_start(nb_t[:], nb)
+        nc.gpsimd.dma_start(gs_t[:], gs.rearrange("(p t) o -> p (t o)", t=PACK))
+        nc.gpsimd.dma_start(gn_t[:], gn.rearrange("(p t) o -> p (t o)", t=PACK))
+        nc.sync.dma_start(w2w_raw[:], words_of(w2_words))
+        for r in range(PACK):
+            nc.sync.dma_start(w2s_raw[r:P:32, :].bitcast(I32), scale_rows(w2_scales, r))
+
+        xs_pick = keep.tile([P, S], U8, align_bytes=64, name="xs_pick")
+        xw_pick = keep.tile([P, S], U32, align_bytes=64, name="xw_pick")
+        ds_pick = keep.tile([P, H], U8, align_bytes=64, name="ds_pick")
+        dw_pick = keep.tile([P, H], U32, align_bytes=64, name="dw_pick")
+        ds_deal = keep.tile([P, H], U8, align_bytes=64, name="ds_deal")
+        dw = keep.tile([P, H], U32, align_bytes=64, name="dw")
+        w1w = keep.tile([P, H], U32, align_bytes=64, name="w1w")
+        w1s = keep.tile([P, H], U8, align_bytes=64, name="w1s")
+        w2w = keep.tile([P, N], U32, align_bytes=64, name="w2w")
+        w2s = keep.tile([P, N], U8, align_bytes=64, name="w2s")
+
+        nc.vector.tensor_copy(xs_pick[:], xs_tab[:].indirect(offs_t[:]))
+        nc.vector.tensor_copy(ds_pick[:], ds_tab[:].indirect(kidx_t[:]))
+        deal(nc, ds_deal[:], ds_pick[:], 16)
+        for r in range(PACK):
+            nc.sync.dma_start(ds_fin[r:P:32, :].bitcast(I32), ds_deal[8 * r : P : 32, :].bitcast(I32))
+        nc.sync.dma_start(res_t[:], res.rearrange("(p t) n -> p t n", t=PACK))
+        nc.vector.tensor_copy(xw_pick[:], xw_tab[:].indirect(offs_t[:]))
+        deal(nc, w1w[:].bitcast(I32), w1w_raw[:], 4)
+        deal(nc, w1s[:], w1s_raw[:], 16)
+
+        y_win = [keep.tile([P, S], F32, name=f"y_win{t}") for t in range(PACK)]
+        y_own = [keep.tile([P, S], F32, name=f"y_own{t}") for t in range(PACK)]
+        y_ps = []
+        for t in range(PACK):
+            cols = slice(t * P, (t + 1) * P)
+            bank = ybank.tile([P, S], F32, name="y_bank")
+            nc.tensor.matmul_mx(
+                out=bank[:], lhsT=w1w[:, cols].bitcast(FP8X4), lhsT_scale=w1s[:, cols],
+                rhs=xw_pick[:].bitcast(FP8X4), rhs_scale=xs_pick[:], start=True, stop=True,
+            )
+            y_ps.append(bank)
+        for half in range(2):
+            cols = slice(half * S // 2, (half + 1) * S // 2)
+            for t in range(PACK):
+                if half == 0:
+                    nc.scalar.activation(out=y_win[t][:], in_=y_ps[t][:], func=ACT.Copy, scale=gs_t[:, t : t + 1])
+                nc.scalar.activation(out=y_own[t][:, cols], in_=y_ps[t][:, cols], func=ACT.Copy, scale=gs_t[:, t : t + 1])
+
+        nc.vector.tensor_copy(dw_pick[:], dw_tab[:].indirect(kidx_t[:]))
+        deal(nc, dw[:].bitcast(I32), dw_pick[:].bitcast(I32), 4)
+        deal(nc, w2w[:].bitcast(I32), w2w_raw[:], 4)
+        deal(nc, w2s[:], w2s_raw[:], 16)
+
+        out_codes = keep.tile([P, S], U32, align_bytes=64, name="out_codes")
+        out_scales = keep.tile([P, S], U8, align_bytes=64, name="out_scales")
+        out_rows = out_0.rearrange("(p t) n -> p t n", t=PACK)
+        state = {}
+
+        def product(bank, words, scales, codes, code_scales):
+            for t in range(PACK):
+                cols = slice(t * P, (t + 1) * P)
+                nc.tensor.matmul_mx(
+                    out=bank[:, t, :], lhsT=words[:, cols].bitcast(FP8X4), lhsT_scale=scales[:, cols],
+                    rhs=codes[:].bitcast(FP8X4), rhs_scale=code_scales[:], start=True, stop=True,
+                )
+
+        def fetch(first, count, tag):
+            diff = keep.tile([P, PACK, count * CH], F32, align_bytes=64, name="diff", tag=tag)
+            for t in range(PACK):
+                nc.vector.tensor_tensor(
+                    diff[:, t, :], y_win[t][:].indirect(nb_t[:, first * LIST_COLS : (first + count) * LIST_COLS]),
+                    y_own[t][:, first * CH : (first + count) * CH], ALU.subtract,
+                )
+            for c in range(count):
+                state["diff", first + c] = diff[:, :, c * CH : (c + 1) * CH]
+
+        def differences(c):
+            if c == 0:
+                fetch(0, 2, "first_half")
+            elif c >= 2:
+                fetch(c, 1, f"z{c - 3}")
+            zq = keep.tile([P, CH, PACK], BF16, align_bytes=64, name="zq", tag=f"z{c}")
+            weave(nc, zq, state["diff", c], -1.0)
+            state["zq", c] = zq
+
+        def scores(c):
+            codes = ring.tile([P, CH], U32, align_bytes=64, name="zq_codes")
+            scales = ring.tile([P, CH], U8, align_bytes=64, name="zq_scales")
+            nc.vector.quantize_mx(out=codes[:].bitcast(FP8X4), scales=scales[:], in_=state["zq", c][:].rearrange("p n t -> p (n t)"))
+            bank = sbank.tile([P, PACK, CH], F32, name="s_bank")
+            product(bank, dw, ds_fin, codes, scales)
+            sig = ring.tile([P, CH, PACK], F32, name="sig")
+            nc.scalar.activation(out=sig[:], in_=bank[:].rearrange("p t n -> p n t"), func=ACT.Sigmoid, scale=0.0625)
+            state["sig", c] = sig
+
+        def weigh(c):
+            z2 = ring.tile([P, CH, PACK], BF16, align_bytes=64, name="z2")
+            nc.vector.tensor_tensor(z2[:], state["sig", c][:], gn_t[:].unsqueeze(1).to_broadcast([P, CH, PACK]), ALU.mult)
+            state["z2", c] = z2
+
+        def values(c):
+            codes = ring.tile([P, CH], U32, align_bytes=64, name="z2_codes")
+            scales = ring.tile([P, CH], U8, align_bytes=64, name="z2_scales")
+            nc.vector.quantize_mx(out=codes[:].bitcast(FP8X4), scales=scales[:], in_=state["z2", c][:].rearrange("p n t -> p (n t)"))
+            bank = obank.tile([P, PACK, CH], F32, name="o_bank")
+            product(bank, w2w, w2s, codes, scales)
+            state["o", c] = bank
+
+        def result(c):
+            cols = slice(c * CH, (c + 1) * CH)
+            total = ring.tile([P, PACK, CH], F32, name="total")
+            nc.vector.tensor_tensor(total[:], state["o", c][:], res_t[:, :, cols], ALU.add)
+            nc.sync.dma_start(out_rows[:, :, cols], total[:])
+            rounded = ring.tile([P, CH, PACK], BF16, align_bytes=64, name="rounded")
+            weave(nc, rounded, total[:], 1.0)
+            state["rounded", c] = rounded
+
+        def planes(c):
+            cols = slice(c * CH, (c + 1) * CH)
+            nc.vector.quantize_mx(
+                out=out_codes[:, cols].bitcast(FP8X4), scales=out_scales[:, cols],
+                in_=state["rounded", c][:].rearrange("p n t -> p (n t)"),
+            )
+            nc.sync.dma_start(words_of(out_1)[:, cols], out_codes[:, cols].bitcast(I32))
+
+        stages = [differences, scores, weigh, values, result, planes]
+        for step in range(CHUNKS + len(stages) - 1):
+            for depth in range(len(stages) - 1, -1, -1):
+                c = step - depth
+                if 0 <= c < CHUNKS:
+                    stages[depth](c)
+        for r in range(PACK):
+            queue = nc.sync if r % 2 == 0 else nc.scalar
+            queue.dma_start(scale_rows(out_2, r), out_scales[r:P:32, :].bitcast(I32))

@@ -26,8 +26,12 @@ def words_of(dram):
     return dram[0].rearrange("p n t -> p (n t)").bitcast(I32)
 
 
-def scale_rows(dram, r):
-    return dram[0].rearrange("(q r) c -> r q c", r=PACK)[r].bitcast(I32)
+def scale_rows(dram, q):
+    return dram[0][PACK * q : PACK * (q + 1), :].bitcast(I32)
+
+
+def live_rows(tile, q, first=0):
+    return tile[32 * q + first : 32 * q + first + PACK, :].bitcast(I32)
 
 
 def deal(nc, dealt, plain, run):
@@ -56,8 +60,7 @@ def tile_picked_pqhop_sigmoid_po_kernel(
         keep = ctx.enter_context(tc.tile_pool(name="keep", bufs=1))
         ring = ctx.enter_context(tc.tile_pool(name="ring", bufs=CHUNKS))
         ybank = ctx.enter_context(tc.psum_pool(name="ybank", bufs=PACK))
-        sbank = ctx.enter_context(tc.psum_pool(name="sbank", bufs=2))
-        obank = ctx.enter_context(tc.psum_pool(name="obank", bufs=2))
+        obank = ctx.enter_context(tc.psum_pool(name="obank", bufs=CHUNKS))
 
         offs_t = lists.tile([P, S // 16], U16, name="offs_t")
         kidx_t = lists.tile([P, H // 16], U16, name="kidx_t")
@@ -66,61 +69,55 @@ def tile_picked_pqhop_sigmoid_po_kernel(
         xs_tab = keep.tile([P, T], U8, align_bytes=64, name="xs_tab")
         ds_tab = keep.tile([P, G], U8, align_bytes=64, name="ds_tab")
         xw_tab = keep.tile([P, T], U32, align_bytes=64, name="xw_tab")
-        dw_tab = keep.tile([P, G], U32, align_bytes=64, name="dw_tab")
+        dw_tab = keep.tile([P, G], U32, align_bytes=64, name="dw_tab", tag="first_half")
         w1w_raw = keep.tile([P, H], I32, align_bytes=64, name="w1w_raw")
         w1s_raw = keep.tile([P, H], U8, align_bytes=64, name="w1s_raw")
         w2w_raw = keep.tile([P, N], I32, align_bytes=64, name="w2w_raw")
-        w2s_raw = keep.tile([P, N], U8, align_bytes=64, name="w2s_raw")
-        ds_fin = keep.tile([P, H], U8, align_bytes=64, name="ds_fin")
+        late_raw = keep.tile([P, N], U8, align_bytes=64, name="late_raw")
         gs_t = keep.tile([P, PACK], F32, name="gs_t")
         gn_t = keep.tile([P, PACK], F32, name="gn_t")
         res_t = keep.tile([P, PACK, S], F32, name="res_t")
-        warm_in = keep.tile([P, 1], F32, name="warm_in")
         warm_out = keep.tile([P, 1], F32, name="warm_out")
 
         nc.gpsimd.memset(xs_tab[:].bitcast(I32), 0)
         nc.vector.memset(ds_tab[:].bitcast(I32), 0)
-        nc.vector.memset(warm_in[:], 0.0)
         nc.vector.memset(w1s_raw[:].bitcast(I32), 0)
-        nc.vector.memset(w2s_raw[:].bitcast(I32), 0)
-        nc.vector.memset(ds_fin[:].bitcast(I32), 0)
-        nc.scalar.activation(out=warm_out[:], in_=warm_in[:], func=ACT.Sigmoid)
+        nc.vector.memset(late_raw[:].bitcast(I32), 0)
 
         nc.sync.dma_start(offs_t[:], offs)
         for r in range(PACK):
-            nc.sync.dma_start(xs_tab[r:P:32, :].bitcast(I32), scale_rows(x_scales, r))
+            queue = nc.sync if r < 2 else nc.scalar
+            queue.dma_start(live_rows(xs_tab, r), scale_rows(x_scales, r))
         nc.sync.dma_start(kidx_t[:], kidx)
         nc.sync.dma_start(ds_tab[0:P:8, :].bitcast(I32), d_scales[0].bitcast(I32))
         nc.sync.dma_start(xw_tab[:].bitcast(I32), words_of(x_words))
-        nc.sync.dma_start(w1w_raw[:], words_of(w1_words))
         for r in range(PACK):
-            nc.sync.dma_start(w1s_raw[r:P:32, :].bitcast(I32), scale_rows(w1_scales, r))
+            nc.sync.dma_start(live_rows(w1s_raw, r), scale_rows(w1_scales, r))
+        nc.sync.dma_start(w1w_raw[:], words_of(w1_words))
         nc.sync.dma_start(dw_tab[:].bitcast(I32), words_of(d_words))
         nc.sync.dma_start(nb_t[:], nb)
         nc.gpsimd.dma_start(gs_t[:], gs.rearrange("(p t) o -> p (t o)", t=PACK))
-        nc.gpsimd.dma_start(gn_t[:], gn.rearrange("(p t) o -> p (t o)", t=PACK))
-        nc.sync.dma_start(w2w_raw[:], words_of(w2_words))
-        for r in range(PACK):
-            nc.sync.dma_start(w2s_raw[r:P:32, :].bitcast(I32), scale_rows(w2_scales, r))
+        nc.scalar.activation(out=warm_out[:], in_=gs_t[:, 0:1], func=ACT.Sigmoid)
 
         xs_pick = keep.tile([P, S], U8, align_bytes=64, name="xs_pick")
-        xw_pick = keep.tile([P, S], U32, align_bytes=64, name="xw_pick")
         ds_pick = keep.tile([P, H], U8, align_bytes=64, name="ds_pick")
         dw_pick = keep.tile([P, H], U32, align_bytes=64, name="dw_pick")
-        ds_deal = keep.tile([P, H], U8, align_bytes=64, name="ds_deal")
         dw = keep.tile([P, H], U32, align_bytes=64, name="dw")
-        w1w = keep.tile([P, H], U32, align_bytes=64, name="w1w")
         w1s = keep.tile([P, H], U8, align_bytes=64, name="w1s")
-        w2w = keep.tile([P, N], U32, align_bytes=64, name="w2w")
-        w2s = keep.tile([P, N], U8, align_bytes=64, name="w2s")
+        late = keep.tile([P, N], U8, align_bytes=64, name="late")
 
         nc.vector.tensor_copy(xs_pick[:], xs_tab[:].indirect(offs_t[:]))
         nc.vector.tensor_copy(ds_pick[:], ds_tab[:].indirect(kidx_t[:]))
-        deal(nc, ds_deal[:], ds_pick[:], 16)
         for r in range(PACK):
-            nc.sync.dma_start(ds_fin[r:P:32, :].bitcast(I32), ds_deal[8 * r : P : 32, :].bitcast(I32))
+            nc.sync.dma_start(live_rows(late_raw, r), ds_pick[32 * r : 32 * (r + 1) : 8, :].bitcast(I32))
+        for r in range(PACK):
+            nc.sync.dma_start(live_rows(late_raw, r, PACK), scale_rows(w2_scales, r))
+        nc.sync.dma_start(gn_t[:], gn.rearrange("(p t) o -> p (t o)", t=PACK))
+        nc.sync.dma_start(w2w_raw[:], words_of(w2_words))
         nc.sync.dma_start(res_t[:], res.rearrange("(p t) n -> p t n", t=PACK))
+        xw_pick = keep.tile([P, S], U32, align_bytes=64, name="xw_pick")
         nc.vector.tensor_copy(xw_pick[:], xw_tab[:].indirect(offs_t[:]))
+        w1w = keep.tile([P, H], U32, align_bytes=64, name="w1w")
         deal(nc, w1w[:].bitcast(I32), w1w_raw[:], 4)
         deal(nc, w1s[:], w1s_raw[:], 16)
 
@@ -129,7 +126,7 @@ def tile_picked_pqhop_sigmoid_po_kernel(
         y_ps = []
         for t in range(PACK):
             cols = slice(t * P, (t + 1) * P)
-            bank = ybank.tile([P, S], F32, name="y_bank")
+            bank = ybank.tile([P, S], F32, name="y_bank", tag="y_then_s")
             nc.tensor.matmul_mx(
                 out=bank[:], lhsT=w1w[:, cols].bitcast(FP8X4), lhsT_scale=w1s[:, cols],
                 rhs=xw_pick[:].bitcast(FP8X4), rhs_scale=xs_pick[:], start=True, stop=True,
@@ -144,19 +141,18 @@ def tile_picked_pqhop_sigmoid_po_kernel(
 
         nc.vector.tensor_copy(dw_pick[:], dw_tab[:].indirect(kidx_t[:]))
         deal(nc, dw[:].bitcast(I32), dw_pick[:].bitcast(I32), 4)
-        deal(nc, w2w[:].bitcast(I32), w2w_raw[:], 4)
-        deal(nc, w2s[:], w2s_raw[:], 16)
+        deal(nc, late[:], late_raw[:], 16)
 
         out_codes = keep.tile([P, S], U32, align_bytes=64, name="out_codes")
         out_scales = keep.tile([P, S], U8, align_bytes=64, name="out_scales")
         out_rows = out_0.rearrange("(p t) n -> p t n", t=PACK)
         state = {}
 
-        def product(bank, words, scales, codes, code_scales):
+        def product(bank, words, first_row, codes, code_scales):
             for t in range(PACK):
                 cols = slice(t * P, (t + 1) * P)
                 nc.tensor.matmul_mx(
-                    out=bank[:, t, :], lhsT=words[:, cols].bitcast(FP8X4), lhsT_scale=scales[:, cols],
+                    out=bank[:, t, :], lhsT=words[:, cols].bitcast(FP8X4), lhsT_scale=late[first_row:P, cols],
                     rhs=codes[:].bitcast(FP8X4), rhs_scale=code_scales[:], start=True, stop=True,
                 )
 
@@ -174,7 +170,7 @@ def tile_picked_pqhop_sigmoid_po_kernel(
             if c == 0:
                 fetch(0, 2, "first_half")
             elif c >= 2:
-                fetch(c, 1, f"z{c - 3}")
+                fetch(c, 1, f"z{c - 2}" if c == CHUNKS - 1 else "third")
             zq = keep.tile([P, CH, PACK], BF16, align_bytes=64, name="zq", tag=f"z{c}")
             weave(nc, zq, state["diff", c], -1.0)
             state["zq", c] = zq
@@ -183,8 +179,8 @@ def tile_picked_pqhop_sigmoid_po_kernel(
             codes = ring.tile([P, CH], U32, align_bytes=64, name="zq_codes")
             scales = ring.tile([P, CH], U8, align_bytes=64, name="zq_scales")
             nc.vector.quantize_mx(out=codes[:].bitcast(FP8X4), scales=scales[:], in_=state["zq", c][:].rearrange("p n t -> p (n t)"))
-            bank = sbank.tile([P, PACK, CH], F32, name="s_bank")
-            product(bank, dw, ds_fin, codes, scales)
+            bank = ybank.tile([P, PACK, CH], F32, name="s_bank", tag="y_then_s")
+            product(bank, dw, 0, codes, scales)
             sig = ring.tile([P, CH, PACK], F32, name="sig")
             nc.scalar.activation(out=sig[:], in_=bank[:].rearrange("p t n -> p n t"), func=ACT.Sigmoid, scale=0.0625)
             state["sig", c] = sig
@@ -199,7 +195,7 @@ def tile_picked_pqhop_sigmoid_po_kernel(
             scales = ring.tile([P, CH], U8, align_bytes=64, name="z2_scales")
             nc.vector.quantize_mx(out=codes[:].bitcast(FP8X4), scales=scales[:], in_=state["z2", c][:].rearrange("p n t -> p (n t)"))
             bank = obank.tile([P, PACK, CH], F32, name="o_bank")
-            product(bank, w2w, w2s, codes, scales)
+            product(bank, state["w2w"], PACK, codes, scales)
             state["o", c] = bank
 
         def result(c):
@@ -208,7 +204,13 @@ def tile_picked_pqhop_sigmoid_po_kernel(
             nc.vector.tensor_tensor(total[:], state["o", c][:], res_t[:, :, cols], ALU.add)
             nc.sync.dma_start(out_rows[:, :, cols], total[:])
             rounded = ring.tile([P, CH, PACK], BF16, align_bytes=64, name="rounded")
-            weave(nc, rounded, total[:], 1.0)
+            if c == CHUNKS - 1:
+                nc.vector.tensor_copy(
+                    out=rounded[:].rearrange("p (c i) t -> p c t i", i=4),
+                    in_=total[:].rearrange("p t (c i) -> p c t i", i=4),
+                )
+            else:
+                weave(nc, rounded, total[:], 1.0)
             state["rounded", c] = rounded
 
         def planes(c):
@@ -219,12 +221,19 @@ def tile_picked_pqhop_sigmoid_po_kernel(
             )
             nc.sync.dma_start(words_of(out_1)[:, cols], out_codes[:, cols].bitcast(I32))
 
-        stages = [differences, scores, weigh, values, result, planes]
-        for step in range(CHUNKS + len(stages) - 1):
-            for depth in range(len(stages) - 1, -1, -1):
-                c = step - depth
-                if 0 <= c < CHUNKS:
-                    stages[depth](c)
+        for c in range(CHUNKS - 1):
+            differences(c)
+        w2w = keep.tile([P, N], U32, align_bytes=64, name="w2w", tag="first_half")
+        state["w2w"] = w2w
+        scores(0)
+        scores(1)
+        differences(CHUNKS - 1)
+        deal(nc, w2w[:].bitcast(I32), w2w_raw[:], 4)
+        scores(2)
+        scores(3)
+        for stage in (weigh, values, result, planes):
+            for c in range(CHUNKS):
+                stage(c)
         for r in range(PACK):
             queue = nc.sync if r % 2 == 0 else nc.scalar
-            queue.dma_start(scale_rows(out_2, r), out_scales[r:P:32, :].bitcast(I32))
+            queue.dma_start(scale_rows(out_2, r), live_rows(out_scales, r))

@@ -98,6 +98,8 @@ def tile_picked_pqhop_sigmoid_po_kernel(
         nc.sync.dma_start(nb_t[:], nb)
         nc.gpsimd.dma_start(gs_t[:], gs.rearrange("(p t) o -> p (t o)", t=PACK))
         nc.scalar.activation(out=warm_out[:], in_=gs_t[:, 0:1], func=ACT.Sigmoid)
+        for r in range(PACK):
+            nc.gpsimd.dma_start(live_rows(late_raw, r, PACK), scale_rows(w2_scales, r))
 
         xs_pick = keep.tile([P, S], U8, align_bytes=64, name="xs_pick")
         ds_pick = keep.tile([P, H], U8, align_bytes=64, name="ds_pick")
@@ -110,8 +112,6 @@ def tile_picked_pqhop_sigmoid_po_kernel(
         nc.vector.tensor_copy(ds_pick[:], ds_tab[:].indirect(kidx_t[:]))
         for r in range(PACK):
             nc.sync.dma_start(live_rows(late_raw, r), ds_pick[32 * r : 32 * (r + 1) : 8, :].bitcast(I32))
-        for r in range(PACK):
-            nc.sync.dma_start(live_rows(late_raw, r, PACK), scale_rows(w2_scales, r))
         nc.sync.dma_start(gn_t[:], gn.rearrange("(p t) o -> p (t o)", t=PACK))
         nc.sync.dma_start(w2w_raw[:], words_of(w2_words))
         nc.sync.dma_start(res_t[:], res.rearrange("(p t) n -> p t n", t=PACK))
@@ -201,25 +201,34 @@ def tile_picked_pqhop_sigmoid_po_kernel(
         def result(c):
             cols = slice(c * CH, (c + 1) * CH)
             total = ring.tile([P, PACK, CH], F32, name="total")
-            nc.vector.tensor_tensor(total[:], state["o", c][:], res_t[:, :, cols], ALU.add)
-            nc.sync.dma_start(out_rows[:, :, cols], total[:])
             rounded = ring.tile([P, CH, PACK], BF16, align_bytes=64, name="rounded")
             if c == CHUNKS - 1:
-                nc.vector.tensor_copy(
-                    out=rounded[:].rearrange("p (c i) t -> p c t i", i=4),
-                    in_=total[:].rearrange("p t (c i) -> p c t i", i=4),
-                )
+                halves = [slice(0, CH // 2), slice(CH // 2, CH)]
+                for h in halves:
+                    nc.vector.tensor_tensor(total[:, :, h], state["o", c][:, :, h], res_t[:, :, cols][:, :, h], ALU.add)
+                for h in halves:
+                    nc.vector.tensor_copy(
+                        out=rounded[:, h, :].rearrange("p (c i) t -> p c t i", i=4),
+                        in_=total[:, :, h].rearrange("p t (c i) -> p c t i", i=4),
+                    )
             else:
+                nc.vector.tensor_tensor(total[:], state["o", c][:], res_t[:, :, cols], ALU.add)
                 weave(nc, rounded, total[:], 1.0)
+            nc.sync.dma_start(out_rows[:, :, cols], total[:])
             state["rounded", c] = rounded
 
         def planes(c):
-            cols = slice(c * CH, (c + 1) * CH)
-            nc.vector.quantize_mx(
-                out=out_codes[:, cols].bitcast(FP8X4), scales=out_scales[:, cols],
-                in_=state["rounded", c][:].rearrange("p n t -> p (n t)"),
-            )
-            nc.sync.dma_start(words_of(out_1)[:, cols], out_codes[:, cols].bitcast(I32))
+            parts = 2 if c == CHUNKS - 1 else 1
+            width = CH // parts
+            for part in range(parts):
+                cols = slice(c * CH + part * width, c * CH + (part + 1) * width)
+                nc.vector.quantize_mx(
+                    out=out_codes[:, cols].bitcast(FP8X4), scales=out_scales[:, cols],
+                    in_=state["rounded", c][:, part * width : (part + 1) * width, :].rearrange("p n t -> p (n t)"),
+                )
+            if c >= CHUNKS - 2:
+                cols = slice(0 if c == CHUNKS - 2 else c * CH, (c + 1) * CH)
+                nc.sync.dma_start(words_of(out_1)[:, cols], out_codes[:, cols].bitcast(I32))
 
         for c in range(CHUNKS - 1):
             differences(c)

from contextlib import ExitStack

import concourse.mybir as mybir

K, T, S, N, H, G = 512, 2048, 512, 512, 512, 2048
FLOPS = 3 * 2 * 512 * 512 * 512

F32 = mybir.dt.float32
BF16 = mybir.dt.bfloat16
I32 = mybir.dt.int32
U32 = mybir.dt.uint32
U16 = mybir.dt.uint16
U8 = mybir.dt.uint8
FP8X4 = mybir.dt.float8_e4m3fn_x4
ACT = mybir.ActivationFunctionType
ALU = mybir.AluOpType

P = 128
PACK = 4
CH = 128
CHUNKS = S // CH
LIST_COLS = CH // 16


def words_of(dram):
    return dram[0].rearrange("p n t -> p (n t)").bitcast(I32)


def scale_rows(dram, q):
    return dram[0][PACK * q : PACK * (q + 1), :].bitcast(I32)


def live_rows(tile, q, first=0):
    return tile[32 * q + first : 32 * q + first + PACK, :].bitcast(I32)


def deal(nc, dealt, plain, run):
    nc.vector.tensor_copy(
        out=dealt.rearrange("p (t c i) -> p c t i", t=PACK, i=run),
        in_=plain.rearrange("p (c i t) -> p c t i", t=PACK, i=run),
    )


def weave(nc, woven, planes, scale):
    nc.scalar.activation(
        out=woven[:].rearrange("p (c i) t -> p c t i", i=4),
        in_=planes.rearrange("p t (c i) -> p c t i", i=4),
        func=ACT.Copy,
        scale=scale,
    )


def tile_picked_pqhop_sigmoid_po_kernel(
    tc, x_words, x_scales, w1_words, w1_scales, gs, d_words, d_scales, gn, res, w2_words, w2_scales, offs, nb, kidx,
    out_0, out_1, out_2,
):
    nc = tc.nc
    with ExitStack() as ctx:
        lists = ctx.enter_context(tc.tile_pool(name="lists", bufs=1))
        keep = ctx.enter_context(tc.tile_pool(name="keep", bufs=1))
        ring = ctx.enter_context(tc.tile_pool(name="ring", bufs=CHUNKS))
        ybank = ctx.enter_context(tc.psum_pool(name="ybank", bufs=PACK))
        obank = ctx.enter_context(tc.psum_pool(name="obank", bufs=CHUNKS))

        offs_t = lists.tile([P, S // 16], U16, name="offs_t")
        kidx_t = lists.tile([P, H // 16], U16, name="kidx_t")
        nb_t = lists.tile([P, S // 16], U16, name="nb_t")

        xs_tab = keep.tile([P, T], U8, align_bytes=64, name="xs_tab")
        ds_tab = keep.tile([P, G], U8, align_bytes=64, name="ds_tab")
        xw_tab = keep.tile([P, T], U32, align_bytes=64, name="xw_tab")
        dw_tab = keep.tile([P, G], U32, align_bytes=64, name="dw_tab", tag="first_half")
        w1w_raw = keep.tile([P, H], I32, align_bytes=64, name="w1w_raw")
        w1s_raw = keep.tile([P, H], U8, align_bytes=64, name="w1s_raw")
        w2w_raw = keep.tile([P, N], I32, align_bytes=64, name="w2w_raw")
        late_raw = keep.tile([P, N], U8, align_bytes=64, name="late_raw")
        gs_t = keep.tile([P, PACK], F32, name="gs_t")
        gn_t = keep.tile([P, PACK], F32, name="gn_t")
        res_t = keep.tile([P, PACK, S], F32, name="res_t")
        warm_out = keep.tile([P, 1], F32, name="warm_out")

        nc.gpsimd.memset(xs_tab[:].bitcast(I32), 0)
        nc.vector.memset(ds_tab[:].bitcast(I32), 0)
        nc.vector.memset(w1s_raw[:].bitcast(I32), 0)
        nc.vector.memset(late_raw[:].bitcast(I32), 0)

        nc.sync.dma_start(offs_t[:], offs)
        for r in range(PACK):
            queue = nc.sync if r < 2 else nc.scalar
            queue.dma_start(live_rows(xs_tab, r), scale_rows(x_scales, r))
        nc.sync.dma_start(kidx_t[:], kidx)
        nc.sync.dma_start(ds_tab[0:P:8, :].bitcast(I32), d_scales[0].bitcast(I32))
        nc.sync.dma_start(xw_tab[:].bitcast(I32), words_of(x_words))
        for r in range(PACK):
            nc.sync.dma_start(live_rows(w1s_raw, r), scale_rows(w1_scales, r))
        nc.sync.dma_start(w1w_raw[:], words_of(w1_words))
        nc.sync.dma_start(dw_tab[:].bitcast(I32), words_of(d_words))
        nc.sync.dma_start(nb_t[:], nb)
        nc.gpsimd.dma_start(gs_t[:], gs.rearrange("(p t) o -> p (t o)", t=PACK))
        nc.scalar.activation(out=warm_out[:], in_=gs_t[:, 0:1], func=ACT.Sigmoid)
        for r in range(PACK):
            nc.gpsimd.dma_start(live_rows(late_raw, r, PACK), scale_rows(w2_scales, r))

        xs_pick = keep.tile([P, S], U8, align_bytes=64, name="xs_pick")
        ds_pick = keep.tile([P, H], U8, align_bytes=64, name="ds_pick")
        dw_pick = keep.tile([P, H], U32, align_bytes=64, name="dw_pick")
        dw = keep.tile([P, H], U32, align_bytes=64, name="dw")
        w1s = keep.tile([P, H], U8, align_bytes=64, name="w1s")
        late = keep.tile([P, N], U8, align_bytes=64, name="late")

        nc.vector.tensor_copy(xs_pick[:], xs_tab[:].indirect(offs_t[:]))
        nc.vector.tensor_copy(ds_pick[:], ds_tab[:].indirect(kidx_t[:]))
        for r in range(PACK):
            nc.sync.dma_start(live_rows(late_raw, r), ds_pick[32 * r : 32 * (r + 1) : 8, :].bitcast(I32))
        nc.sync.dma_start(gn_t[:], gn.rearrange("(p t) o -> p (t o)", t=PACK))
        nc.sync.dma_start(w2w_raw[:], words_of(w2_words))
        nc.sync.dma_start(res_t[:], res.rearrange("(p t) n -> p t n", t=PACK))
        xw_pick = keep.tile([P, S], U32, align_bytes=64, name="xw_pick")
        nc.vector.tensor_copy(xw_pick[:], xw_tab[:].indirect(offs_t[:]))
        w1w = keep.tile([P, H], U32, align_bytes=64, name="w1w")
        deal(nc, w1w[:].bitcast(I32), w1w_raw[:], 4)
        deal(nc, w1s[:], w1s_raw[:], 16)

        y_win = [keep.tile([P, S], F32, name=f"y_win{t}") for t in range(PACK)]
        y_own = [keep.tile([P, S], F32, name=f"y_own{t}") for t in range(PACK)]
        y_ps = []
        for t in range(PACK):
            cols = slice(t * P, (t + 1) * P)
            bank = ybank.tile([P, S], F32, name="y_bank", tag="y_then_s")
            nc.tensor.matmul_mx(
                out=bank[:], lhsT=w1w[:, cols].bitcast(FP8X4), lhsT_scale=w1s[:, cols],
                rhs=xw_pick[:].bitcast(FP8X4), rhs_scale=xs_pick[:], start=True, stop=True,
            )
            y_ps.append(bank)
        for half in range(2):
            cols = slice(half * S // 2, (half + 1) * S // 2)
            for t in range(PACK):
                if half == 0:
                    nc.scalar.activation(out=y_win[t][:], in_=y_ps[t][:], func=ACT.Copy, scale=gs_t[:, t : t + 1])
                nc.scalar.activation(out=y_own[t][:, cols], in_=y_ps[t][:, cols], func=ACT.Copy, scale=gs_t[:, t : t + 1])

        nc.vector.tensor_copy(dw_pick[:], dw_tab[:].indirect(kidx_t[:]))
        deal(nc, dw[:].bitcast(I32), dw_pick[:].bitcast(I32), 4)
        deal(nc, late[:], late_raw[:], 16)

        out_codes = keep.tile([P, S], U32, align_bytes=64, name="out_codes")
        out_scales = keep.tile([P, S], U8, align_bytes=64, name="out_scales")
        out_rows = out_0.rearrange("(p t) n -> p t n", t=PACK)
        state = {}

        def product(bank, words, first_row, codes, code_scales):
            for t in range(PACK):
                cols = slice(t * P, (t + 1) * P)
                nc.tensor.matmul_mx(
                    out=bank[:, t, :], lhsT=words[:, cols].bitcast(FP8X4), lhsT_scale=late[first_row:P, cols],
                    rhs=codes[:].bitcast(FP8X4), rhs_scale=code_scales[:], start=True, stop=True,
                )

        def fetch(first, count, tag):
            diff = keep.tile([P, PACK, count * CH], F32, align_bytes=64, name="diff", tag=tag)
            for t in range(PACK):
                nc.vector.tensor_tensor(
                    diff[:, t, :], y_win[t][:].indirect(nb_t[:, first * LIST_COLS : (first + count) * LIST_COLS]),
                    y_own[t][:, first * CH : (first + count) * CH], ALU.subtract,
                )
            for c in range(count):
                state["diff", first + c] = diff[:, :, c * CH : (c + 1) * CH]

        def differences(c):
            if c == 0:
                fetch(0, 2, "first_half")
            elif c >= 2:
                fetch(c, 1, f"z{c - 2}" if c == CHUNKS - 1 else "third")
            zq = keep.tile([P, CH, PACK], BF16, align_bytes=64, name="zq", tag=f"z{c}")
            weave(nc, zq, state["diff", c], -1.0)
            state["zq", c] = zq

        def scores(c):
            codes = ring.tile([P, CH], U32, align_bytes=64, name="zq_codes")
            scales = ring.tile([P, CH], U8, align_bytes=64, name="zq_scales")
            nc.vector.quantize_mx(out=codes[:].bitcast(FP8X4), scales=scales[:], in_=state["zq", c][:].rearrange("p n t -> p (n t)"))
            bank = ybank.tile([P, PACK, CH], F32, name="s_bank", tag="y_then_s")
            product(bank, dw, 0, codes, scales)
            sig = ring.tile([P, CH, PACK], F32, name="sig")
            nc.scalar.activation(out=sig[:], in_=bank[:].rearrange("p t n -> p n t"), func=ACT.Sigmoid, scale=0.0625)
            state["sig", c] = sig

        def weigh(c):
            z2 = ring.tile([P, CH, PACK], BF16, align_bytes=64, name="z2")
            nc.vector.tensor_tensor(z2[:], state["sig", c][:], gn_t[:].unsqueeze(1).to_broadcast([P, CH, PACK]), ALU.mult)
            state["z2", c] = z2

        def values(c):
            codes = ring.tile([P, CH], U32, align_bytes=64, name="z2_codes")
            scales = ring.tile([P, CH], U8, align_bytes=64, name="z2_scales")
            nc.vector.quantize_mx(out=codes[:].bitcast(FP8X4), scales=scales[:], in_=state["z2", c][:].rearrange("p n t -> p (n t)"))
            bank = obank.tile([P, PACK, CH], F32, name="o_bank")
            product(bank, state["w2w"], PACK, codes, scales)
            state["o", c] = bank

        def result(c):
            cols = slice(c * CH, (c + 1) * CH)
            total = ring.tile([P, PACK, CH], F32, name="total")
            rounded = ring.tile([P, CH, PACK], BF16, align_bytes=64, name="rounded")
            if c == CHUNKS - 1:
                halves = [slice(0, CH // 2), slice(CH // 2, CH)]
                for h in halves:
                    nc.vector.tensor_tensor(total[:, :, h], state["o", c][:, :, h], res_t[:, :, cols][:, :, h], ALU.add)
                for h in halves:
                    nc.vector.tensor_copy(
                        out=rounded[:, h, :].rearrange("p (c i) t -> p c t i", i=4),
                        in_=total[:, :, h].rearrange("p t (c i) -> p c t i", i=4),
                    )
            else:
                nc.vector.tensor_tensor(total[:], state["o", c][:], res_t[:, :, cols], ALU.add)
                weave(nc, rounded, total[:], 1.0)
            nc.sync.dma_start(out_rows[:, :, cols], total[:])
            state["rounded", c] = rounded

        def planes(c):
            parts = 2 if c == CHUNKS - 1 else 1
            width = CH // parts
            for part in range(parts):
                cols = slice(c * CH + part * width, c * CH + (part + 1) * width)
                nc.vector.quantize_mx(
                    out=out_codes[:, cols].bitcast(FP8X4), scales=out_scales[:, cols],
                    in_=state["rounded", c][:, part * width : (part + 1) * width, :].rearrange("p n t -> p (n t)"),
                )
            if c >= CHUNKS - 2:
                cols = slice(0 if c == CHUNKS - 2 else c * CH, (c + 1) * CH)
                nc.sync.dma_start(words_of(out_1)[:, cols], out_codes[:, cols].bitcast(I32))

        for c in range(CHUNKS - 1):
            differences(c)
        w2w = keep.tile([P, N], U32, align_bytes=64, name="w2w", tag="first_half")
        state["w2w"] = w2w
        scores(0)
        scores(1)
        differences(CHUNKS - 1)
        deal(nc, w2w[:].bitcast(I32), w2w_raw[:], 4)
        scores(2)
        scores(3)
        for stage in (weigh, values, result, planes):
            for c in range(CHUNKS):
                stage(c)
        for r in range(PACK):
            queue = nc.sync if r % 2 == 0 else nc.scalar
            queue.dma_start(scale_rows(out_2, r), live_rows(out_scales, r))
